import numpy as np
import ml_dtypes


def mxq(x, axis, fmt="e4m3"):
    dtype, down = {"e4m3": (ml_dtypes.float8_e4m3fn, 7), "e5m2": (ml_dtypes.float8_e5m2, 14)}[fmt]
    v = np.moveaxis(np.asarray(x, np.float32).astype(ml_dtypes.bfloat16).astype(np.float64), axis, -1)
    blocks = v.reshape(v.shape[:-1] + (-1, 32))
    amax = np.abs(blocks).max(-1, keepdims=True)
    byte = np.maximum(np.where(amax > 0, np.frexp(amax)[1] - 1 + 127, 0) - down, 1)
    scale = np.exp2(byte - 127.0)
    codes = (blocks / scale).astype(np.float32).astype(dtype).astype(np.float64)
    return np.moveaxis((codes * scale).reshape(v.shape), -1, axis)


WIDE = False


def mx_kscale(k):
    if not WIDE:
        return np.ones(k)
    levels = np.array([10, -10, 5, -5, 0])
    if k % 512:
        return np.exp2(np.random.permutation(np.resize(levels, k // 32))).repeat(32)
    a = np.empty((k // 512, 16))
    for p in range(k // 512):
        a[p, :8] = np.random.permutation(np.resize(levels, 8))
        for g in range(8):
            far = levels[np.abs(levels - a[p, g]) >= 10]
            a[p, g + 8] = far[np.random.randint(len(far))]
    return np.exp2(a.ravel()).repeat(32)


def f64(x):
    return np.asarray(x).astype(np.float64)


def striped(idx):
    return np.tile(idx.reshape(-1, 16).T, (8, 1)).astype(np.uint16)


def unstriped(offs):
    return offs[:16].T.reshape(-1).astype(np.int64)


def striped8(idx):
    return np.concatenate([x.reshape(-1, 16).T for x in idx]).astype(np.uint16)


def runs(offs, k):
    lists = np.stack([offs[16 * r : 16 * r + 16].T.reshape(-1) for r in range(8)]).astype(np.int64)
    return lists[np.arange(k) % 512 // 64]


def pack_weight(w):
    k, n = w.shape
    w = f64(np.asarray(w, np.float32).astype(ml_dtypes.bfloat16)).reshape(k // 32, 32, n)
    amax = np.abs(w).max(1)
    byte = np.clip(np.where(amax > 0, np.frexp(amax)[1] - 1 + 127 - 7, 1), 1, 254)
    scaled = (w * np.exp2(127.0 - byte)[:, None, :]).reshape(k, n).astype(np.float32)
    words = np.ascontiguousarray(scaled.reshape(k // 512, 128, 4, n).transpose(0, 1, 3, 2)).astype(ml_dtypes.float8_e4m3fn).view(np.uint8)
    return words, np.ascontiguousarray(byte.astype(np.uint8).reshape(k // 512, 16, n))


def unpack_weight(words, scales):
    g, p, n, _ = words.shape
    vals = np.ascontiguousarray(words).view(ml_dtypes.float8_e4m3fn).astype(np.float64) * np.repeat(np.exp2(scales.astype(np.float64) - 127.0), 8, axis=1)[..., None]
    return vals.transpose(0, 1, 3, 2).reshape(g * 512, n)


def relu(v):
    return np.maximum(v, 0.0)


K, T, S, N, H, U = 512, 2048, 256, 512, 512, 1024


def setup_inputs():
    n = np.random.standard_normal
    s = mx_kscale(K)[:, None]
    u = mx_kscale(H)
    packed_xT = pack_weight(n((K, T)) * s)
    packed_w1 = pack_weight(n((K, H)) / np.sqrt(2 * K) / s)
    packed_w2 = pack_weight(n((K, H)) / np.sqrt(2 * K) / s)
    packed_w3 = pack_weight(n((H, N)) / np.sqrt(H) / u[:, None])
    return {
        "x_words": packed_xT[0],
        "x_scales": packed_xT[1],
        "w1_words": packed_w1[0],
        "w1_scales": packed_w1[1],
        "w2_words": packed_w2[0],
        "w2_scales": packed_w2[1],
        "gn": (np.random.uniform(0.5, 1.5, (H, 1)) * u[:, None]).astype(np.float32),
        "w3_words": packed_w3[0],
        "w3_scales": packed_w3[1],
        "offs": striped8(np.random.randint(0, T, (8, S))),
        "hz": striped8(np.random.randint(0, T, (8, S))),
        "n1": striped(np.random.permutation(S)),
        "n2": striped(np.random.permutation(U)[:S]),
        "n3": striped(np.random.permutation(S)),
    }


def reference(x_words, x_scales, w1_words, w1_scales, w2_words, w2_scales, gn, w3_words, w3_scales, offs, hz, n1, n2, n3):
    xq = unpack_weight(x_words, x_scales)[np.arange(K)[:, None], runs(offs, K)]
    x_hz = unpack_weight(x_words, x_scales)[np.arange(K)[:, None], runs(hz, K)]
    y = unpack_weight(w1_words, w1_scales).T @ xq + unpack_weight(w2_words, w2_scales).T @ x_hz
    ds = np.zeros((H, S))
    ds[:, unstriped(n1)] = y
    z = f64(gn) * (y - ds)
    h = unpack_weight(w3_words, w3_scales).T @ mxq(z, 0, "e4m3")
    nw = h - (relu(h[:, unstriped(n3)]))
    out = np.zeros((N, U))
    out[:, unstriped(n2)] = nw
    return out

@@ -1,0 +1,172 @@
+from contextlib import ExitStack
+
+import concourse.mybir as mybir
+
+K, T, S, N, H, U = 512, 2048, 256, 512, 512, 1024
+FLOPS = 2 * (2 * K * H * S + H * N * S)
+
+F32 = mybir.dt.float32
+BF16 = mybir.dt.bfloat16
+I32 = mybir.dt.int32
+U32 = mybir.dt.uint32
+U16 = mybir.dt.uint16
+U8 = mybir.dt.uint8
+FP8X4 = mybir.dt.float8_e4m3fn_x4
+ALU = mybir.AluOpType
+ACT = mybir.ActivationFunctionType
+
+P = 128
+PACK = 4
+QUAD = 32
+STAGE_STEP = 8
+SEND_WINDOW = 2 * S
+FETCH_WINDOW = S + 16
+
+
+def words_of(packed):
+    return packed[0].rearrange("p n t -> p (n t)").bitcast(I32)
+
+
+def tile_picked_dhlsendmxpagez_none_p_kernel(
+    tc, x_words, x_scales, w1_words, w1_scales, w2_words, w2_scales, gn, w3_words, w3_scales, offs, hz, n1, n2, n3, out
+):
+    nc = tc.nc
+    with ExitStack() as ctx:
+        lists = ctx.enter_context(tc.tile_pool(name="lists", bufs=1))
+        keep = ctx.enter_context(tc.tile_pool(name="keep", bufs=1))
+        psum = ctx.enter_context(tc.psum_pool(name="psum", bufs=1))
+
+        def load_list(name, src):
+            tile = lists.tile([P, S // 16], U16, name=name)
+            nc.sync.dma_start(tile[:], src)
+            return tile
+
+        x_scale_table = keep.tile([P, T], U8, name="x_scale_table", align_bytes=64)
+        w_scale_raw = keep.tile([P, 2 * H], U8, name="w_scale_raw", align_bytes=64)
+        w3_scale = keep.tile([P, N], U8, name="w3_scale", align_bytes=64)
+        nc.vector.memset(x_scale_table[:].bitcast(I32), 0)
+        nc.vector.memset(w_scale_raw[:].bitcast(I32), 0)
+        nc.vector.memset(w3_scale[:].bitcast(I32), 0)
+
+        x_table = keep.tile([P, T], U32, name="x_table", align_bytes=64)
+        nc.scalar.dma_start(x_table[:].bitcast(I32), words_of(x_words))
+        pick_lists = [load_list("offs_list", offs), load_list("hz_list", hz)]
+        nc.sync.dma_start(x_scale_table[0:P:STAGE_STEP, :].bitcast(I32), x_scales[0].bitcast(I32))
+        for w, scales in enumerate((w1_scales, w2_scales)):
+            nc.sync.dma_start(w_scale_raw[0:P:STAGE_STEP, w * H : (w + 1) * H].bitcast(I32), scales[0].bitcast(I32))
+        send_list = load_list("n1_list", n1)
+        fetch_list = load_list("n3_list", n3)
+        page_list = load_list("n2_list", n2)
+
+        gain = keep.tile([P, PACK], F32, name="gain")
+        nc.gpsimd.dma_start(gain[:], gn.rearrange("(p t) o -> p (t o)", t=PACK))
+        w_raw = []
+        for w, words in enumerate((w1_words, w2_words)):
+            raw = keep.tile([P, H], U32, name=f"w_raw{w}", tag=f"w_raw{w}", align_bytes=64)
+            nc.gpsimd.dma_start(raw[:].bitcast(I32), words_of(words))
+            w_raw.append(raw)
+        for a in range(PACK):
+            nc.gpsimd.dma_start(w3_scale[a:P:QUAD, :].bitcast(I32), w3_scales[0, a : 16 : PACK, :].bitcast(I32))
+        pages, fetch_from = [], []
+        for t in range(N // P):
+            page = keep.tile([P, U], F32, name=f"page{t}")
+            nc.gpsimd.memset(page[:], 0.0)
+            pages.append(page)
+            positive = keep.tile([P, FETCH_WINDOW], F32, name=f"positive{t}")
+            nc.vector.memset(positive[:, S:], 0.0)
+            fetch_from.append(positive)
+
+        minus_gain = keep.tile([P, PACK], F32, name="minus_gain")
+        nc.scalar.activation(minus_gain[:], gain[:], ACT.Copy, scale=-1.0)
+
+        picked_scale = keep.tile([P, 2 * S], U8, name="picked_scale", align_bytes=64)
+        for w in range(2):
+            nc.vector.tensor_copy(picked_scale[:, w * S : (w + 1) * S], x_scale_table[:].indirect(pick_lists[w][:]))
+        x_scale = keep.tile([P, 2 * S], U8, name="x_scale", align_bytes=64)
+        nc.vector.tensor_copy(x_scale[:].bitcast(I32), picked_scale[:].bitcast(I32))
+        for a in range(1, PACK):
+            nc.sync.dma_start(x_scale[a:P:QUAD, :].bitcast(I32), picked_scale[STAGE_STEP * a : P : QUAD, :].bitcast(I32))
+
+        w_scale = keep.tile([P, 2 * H], U8, name="w_scale", align_bytes=64)
+        nc.vector.tensor_copy(
+            w_scale[:].rearrange("p (w t m) -> p w m t", w=2, t=PACK),
+            w_scale_raw[:].rearrange("p (w m t) -> p w m t", w=2, t=PACK),
+        )
+        for a in range(1, PACK):
+            nc.sync.dma_start(w_scale[a:P:QUAD, :].bitcast(I32), w_scale[STAGE_STEP * a : P : QUAD, :].bitcast(I32))
+
+        picked = []
+        for w in range(2):
+            tile = keep.tile([P, S], U32, name=f"picked{w}", align_bytes=64)
+            nc.vector.tensor_copy(tile[:], x_table[:].indirect(pick_lists[w][:]))
+            picked.append(tile)
+
+        w_codes = []
+        for w in range(2):
+            dealt = keep.tile([P, H], U32, name=f"w_codes{w}", align_bytes=64)
+            nc.scalar.copy(
+                dealt[:].rearrange("p (t m) -> p m t", t=PACK), w_raw[w][:].rearrange("p (m t) -> p m t", t=PACK)
+            )
+            w_codes.append(dealt)
+        w3_codes = keep.tile([P, N], U32, name="w3_codes", tag="w_raw0", align_bytes=64)
+        nc.sync.dma_start(w3_codes[:].bitcast(I32), words_of(w3_words))
+
+        y_banks = [psum.tile([P, S], F32, name=f"y_bank{t}") for t in range(PACK)]
+        for t in range(PACK):
+            for w in range(2):
+                nc.tensor.matmul_mx(
+                    out=y_banks[t][:],
+                    lhsT=w_codes[w][:, t * P : (t + 1) * P].bitcast(FP8X4),
+                    lhsT_scale=w_scale[:, w * H + t * P : w * H + (t + 1) * P],
+                    rhs=picked[w][:].bitcast(FP8X4),
+                    rhs_scale=x_scale[:, w * S : (w + 1) * S],
+                    start=(w == 0),
+                    stop=(w == 1),
+                )
+
+        z_words = keep.tile([P, S, PACK], BF16, name="z_words", align_bytes=64)
+        y_rows, y_gained, sent = [], [], []
+        for t in range(PACK):
+            y = keep.tile([P, S], F32, name=f"y{t}")
+            nc.vector.tensor_copy(y[:], y_banks[t][:])
+            ds = keep.tile([P, SEND_WINDOW], F32, name=f"ds{t}")
+            nc.scalar.activation(ds[:].indirect(send_list[:]), y[:], ACT.Copy)
+            y_rows.append(y)
+            sent.append(ds)
+        for t in range(PACK):
+            gained = keep.tile([P, S], F32, name=f"gained{t}")
+            nc.vector.tensor_scalar(gained[:], y_banks[t][:], gain[:, t : t + 1], None, ALU.mult)
+            y_gained.append(gained)
+        for t in range(PACK):
+            nc.vector.scalar_tensor_tensor(
+                z_words[:, :, t], sent[t][:, :S], minus_gain[:, t : t + 1], y_gained[t][:], ALU.mult, ALU.add
+            )
+
+        z_codes = keep.tile([P, S], U32, name="z_codes", align_bytes=64)
+        z_scale = keep.tile([P, S], U8, name="z_scale", align_bytes=64)
+        nc.vector.quantize_mx(
+            out=z_codes[:].bitcast(FP8X4), scales=z_scale[:], in_=z_words[:].rearrange("p j t -> p (j t)")
+        )
+
+        h_banks = [psum.tile([P, S], F32, name=f"h_bank{t}") for t in range(N // P)]
+        for t in range(N // P):
+            nc.tensor.matmul_mx(
+                out=h_banks[t][:],
+                lhsT=w3_codes[:, t * P : (t + 1) * P].bitcast(FP8X4),
+                lhsT_scale=w3_scale[:, t * P : (t + 1) * P],
+                rhs=z_codes[:].bitcast(FP8X4),
+                rhs_scale=z_scale[:],
+                start=True,
+                stop=True,
+            )
+        fetched = []
+        for t in range(N // P):
+            nc.vector.tensor_scalar(fetch_from[t][:, :S], h_banks[t][:], 0.0, None, ALU.max)
+            got = keep.tile([P, S], F32, name=f"fetched{t}")
+            nc.scalar.activation(got[:], fetch_from[t][:].indirect(fetch_list[:]), ACT.Copy)
+            fetched.append(got)
+        for t in range(N // P):
+            nw = keep.tile([P, S], F32, name=f"nw{t}")
+            nc.vector.tensor_tensor(nw[:], h_banks[t][:], fetched[t][:], ALU.subtract)
+            nc.scalar.activation(pages[t][:].indirect(page_list[:]), nw[:], ACT.Copy)
+            nc.sync.dma_start(out[t * P : (t + 1) * P, :], pages[t][:])

@@ -21,6 +21,10 @@ QUAD = 32
 STAGE_STEP = 8
 SEND_WINDOW = 2 * S
 FETCH_WINDOW = S + 16
+PAGE_BYTES = 4 * U
+WHOLE = (slice(0, S),)
+HALVES = (slice(0, S // 2), slice(S // 2, S))
+Z_CODE_BYTES = 4 * S
 
 
 def words_of(packed):
@@ -34,6 +38,7 @@ def tile_picked_dhlsendmxpagez_none_p_kernel(
     with ExitStack() as ctx:
         lists = ctx.enter_context(tc.tile_pool(name="lists", bufs=1))
         keep = ctx.enter_context(tc.tile_pool(name="keep", bufs=1))
+        shared = ctx.enter_context(tc.tile_pool(name="shared", bufs=1))
         psum = ctx.enter_context(tc.psum_pool(name="psum", bufs=1))
 
         def load_list(name, src):
@@ -42,42 +47,37 @@ def tile_picked_dhlsendmxpagez_none_p_kernel(
             return tile
 
         x_scale_table = keep.tile([P, T], U8, name="x_scale_table", align_bytes=64)
-        w_scale_raw = keep.tile([P, 2 * H], U8, name="w_scale_raw", align_bytes=64)
-        w3_scale = keep.tile([P, N], U8, name="w3_scale", align_bytes=64)
+        w_scale_raw = keep.tile([P, 2 * H], U8, name="w_scale_raw", tag="w_scale_raw", align_bytes=64)
         nc.vector.memset(x_scale_table[:].bitcast(I32), 0)
         nc.vector.memset(w_scale_raw[:].bitcast(I32), 0)
-        nc.vector.memset(w3_scale[:].bitcast(I32), 0)
+        zero = keep.tile([P, 1], F32, name="zero")
+        nc.vector.memset(zero[:], 0.0)
 
         x_table = keep.tile([P, T], U32, name="x_table", align_bytes=64)
-        nc.scalar.dma_start(x_table[:].bitcast(I32), words_of(x_words))
         pick_lists = [load_list("offs_list", offs), load_list("hz_list", hz)]
         nc.sync.dma_start(x_scale_table[0:P:STAGE_STEP, :].bitcast(I32), x_scales[0].bitcast(I32))
         for w, scales in enumerate((w1_scales, w2_scales)):
             nc.sync.dma_start(w_scale_raw[0:P:STAGE_STEP, w * H : (w + 1) * H].bitcast(I32), scales[0].bitcast(I32))
         send_list = load_list("n1_list", n1)
         fetch_list = load_list("n3_list", n3)
+        nc.sync.dma_start(x_table[:].bitcast(I32), words_of(x_words))
         page_list = load_list("n2_list", n2)
-
         gain = keep.tile([P, PACK], F32, name="gain")
         nc.gpsimd.dma_start(gain[:], gn.rearrange("(p t) o -> p (t o)", t=PACK))
         w_raw = []
         for w, words in enumerate((w1_words, w2_words)):
             raw = keep.tile([P, H], U32, name=f"w_raw{w}", tag=f"w_raw{w}", align_bytes=64)
-            nc.gpsimd.dma_start(raw[:].bitcast(I32), words_of(words))
+            nc.sync.dma_start(raw[:].bitcast(I32), words_of(words))
             w_raw.append(raw)
-        for a in range(PACK):
-            nc.gpsimd.dma_start(w3_scale[a:P:QUAD, :].bitcast(I32), w3_scales[0, a : 16 : PACK, :].bitcast(I32))
-        pages, fetch_from = [], []
+
+        first_page = keep.tile([P, U], F32, name="page0")
+        nc.scalar.activation(first_page[:], zero[:, 0:1].to_broadcast([P, U]), ACT.Copy)
+        fetch_from = []
         for t in range(N // P):
-            page = keep.tile([P, U], F32, name=f"page{t}")
-            nc.gpsimd.memset(page[:], 0.0)
-            pages.append(page)
             positive = keep.tile([P, FETCH_WINDOW], F32, name=f"positive{t}")
             nc.vector.memset(positive[:, S:], 0.0)
             fetch_from.append(positive)
 
-        minus_gain = keep.tile([P, PACK], F32, name="minus_gain")
-        nc.scalar.activation(minus_gain[:], gain[:], ACT.Copy, scale=-1.0)
 
         picked_scale = keep.tile([P, 2 * S], U8, name="picked_scale", align_bytes=64)
         for w in range(2):
@@ -102,16 +102,23 @@ def tile_picked_dhlsendmxpagez_none_p_kernel(
             picked.append(tile)
 
         w_codes = []
-        for w in range(2):
+        for w, (copy, word) in enumerate(((nc.scalar.copy, U32), (nc.vector.tensor_copy, I32))):
             dealt = keep.tile([P, H], U32, name=f"w_codes{w}", align_bytes=64)
-            nc.scalar.copy(
-                dealt[:].rearrange("p (t m) -> p m t", t=PACK), w_raw[w][:].rearrange("p (m t) -> p m t", t=PACK)
+            copy(
+                dealt[:].bitcast(word).rearrange("p (t m) -> p m t", t=PACK),
+                w_raw[w][:].bitcast(word).rearrange("p (m t) -> p m t", t=PACK),
             )
             w_codes.append(dealt)
         w3_codes = keep.tile([P, N], U32, name="w3_codes", tag="w_raw0", align_bytes=64)
+        minus_gain = keep.tile([P, PACK], F32, name="minus_gain")
+        nc.vector.tensor_scalar(minus_gain[:], gain[:], -1.0, None, ALU.mult)
+        w3_scale = keep.tile([P, N], U8, name="w3_scale", tag="w_scale_raw", align_bytes=64)
+        nc.vector.memset(w3_scale[:].bitcast(I32), 0)
+        for a in range(PACK):
+            nc.sync.dma_start(w3_scale[a:P:QUAD, :].bitcast(I32), w3_scales[0, a : 16 : PACK, :].bitcast(I32))
         nc.sync.dma_start(w3_codes[:].bitcast(I32), words_of(w3_words))
 
-        y_banks = [psum.tile([P, S], F32, name=f"y_bank{t}") for t in range(PACK)]
+        y_banks = [psum.tile([P, S], F32, name=f"y_bank{t}", tag=f"y_bank{t}") for t in range(PACK)]
         for t in range(PACK):
             for w in range(2):
                 nc.tensor.matmul_mx(
@@ -138,35 +145,56 @@ def tile_picked_dhlsendmxpagez_none_p_kernel(
             nc.vector.tensor_scalar(gained[:], y_banks[t][:], gain[:, t : t + 1], None, ALU.mult)
             y_gained.append(gained)
         for t in range(PACK):
-            nc.vector.scalar_tensor_tensor(
-                z_words[:, :, t], sent[t][:, :S], minus_gain[:, t : t + 1], y_gained[t][:], ALU.mult, ALU.add
+            for cols in HALVES if t == PACK - 1 else WHOLE:
+                nc.vector.scalar_tensor_tensor(
+                    z_words[:, cols, t], sent[t][:, cols], minus_gain[:, t : t + 1], y_gained[t][:, cols], ALU.mult, ALU.add
+                )
+
+        z_codes = shared.tile([P, S], U32, name="z_codes", align_bytes=64, offset=PAGE_BYTES - Z_CODE_BYTES // 2)
+        z_scale = shared.tile([P, S], U8, name="z_scale", align_bytes=64, offset=2 * PAGE_BYTES)
+        for cols in HALVES:
+            nc.vector.quantize_mx(
+                out=z_codes[:, cols].bitcast(FP8X4),
+                scales=z_scale[:, cols],
+                in_=z_words[:, cols, :].rearrange("p j t -> p (j t)"),
             )
 
-        z_codes = keep.tile([P, S], U32, name="z_codes", align_bytes=64)
-        z_scale = keep.tile([P, S], U8, name="z_scale", align_bytes=64)
-        nc.vector.quantize_mx(
-            out=z_codes[:].bitcast(FP8X4), scales=z_scale[:], in_=z_words[:].rearrange("p j t -> p (j t)")
-        )
-
-        h_banks = [psum.tile([P, S], F32, name=f"h_bank{t}") for t in range(N // P)]
+        h_parts = []
         for t in range(N // P):
-            nc.tensor.matmul_mx(
-                out=h_banks[t][:],
-                lhsT=w3_codes[:, t * P : (t + 1) * P].bitcast(FP8X4),
-                lhsT_scale=w3_scale[:, t * P : (t + 1) * P],
-                rhs=z_codes[:].bitcast(FP8X4),
-                rhs_scale=z_scale[:],
-                start=True,
-                stop=True,
-            )
+            parts = []
+            for cols in HALVES if t == 0 else WHOLE:
+                tag = "y_bank0" if cols.start else f"h_bank{t}"
+                bank = psum.tile([P, cols.stop - cols.start], F32, name=f"h{t}_{cols.start}", tag=tag)
+                nc.tensor.matmul_mx(
+                    out=bank[:],
+                    lhsT=w3_codes[:, t * P : (t + 1) * P].bitcast(FP8X4),
+                    lhsT_scale=w3_scale[:, t * P : (t + 1) * P],
+                    rhs=z_codes[:, cols].bitcast(FP8X4),
+                    rhs_scale=z_scale[:, cols],
+                    start=True,
+                    stop=True,
+                )
+                parts.append((cols, bank))
+            h_parts.append(parts)
         fetched = []
         for t in range(N // P):
-            nc.vector.tensor_scalar(fetch_from[t][:, :S], h_banks[t][:], 0.0, None, ALU.max)
+            for cols, bank in h_parts[t]:
+                nc.vector.tensor_scalar(fetch_from[t][:, cols], bank[:], 0.0, None, ALU.max)
             got = keep.tile([P, S], F32, name=f"fetched{t}")
             nc.scalar.activation(got[:], fetch_from[t][:].indirect(fetch_list[:]), ACT.Copy)
             fetched.append(got)
+        results = []
         for t in range(N // P):
             nw = keep.tile([P, S], F32, name=f"nw{t}")
-            nc.vector.tensor_tensor(nw[:], h_banks[t][:], fetched[t][:], ALU.subtract)
+            for cols, bank in h_parts[t]:
+                nc.vector.tensor_tensor(nw[:, cols], bank[:], fetched[t][:, cols], ALU.subtract)
+            results.append(nw)
+        pages = [first_page]
+        for t in range(1, N // P):
+            page = shared.tile([P, U], F32, name=f"page{t}", align_bytes=64, offset=(t - 1) * PAGE_BYTES)
+            nc.vector.memset(page[:], 0.0)
+            pages.append(page)
+        for t in range(N // P):
+            nw = results[t]
             nc.scalar.activation(pages[t][:].indirect(page_list[:]), nw[:], ACT.Copy)
             nc.sync.dma_start(out[t * P : (t + 1) * P, :], pages[t][:])

@@ -19,12 +19,12 @@ P = 128
 PACK = 4
 QUAD = 32
 STAGE_STEP = 8
+GROUP = 16
+EARLY_PAGES = 2
 SEND_WINDOW = 2 * S
 FETCH_WINDOW = S + 16
-PAGE_BYTES = 4 * U
 WHOLE = (slice(0, S),)
 HALVES = (slice(0, S // 2), slice(S // 2, S))
-Z_CODE_BYTES = 4 * S
 
 
 def words_of(packed):
@@ -38,7 +38,6 @@ def tile_picked_dhlsendmxpagez_none_p_kernel(
     with ExitStack() as ctx:
         lists = ctx.enter_context(tc.tile_pool(name="lists", bufs=1))
         keep = ctx.enter_context(tc.tile_pool(name="keep", bufs=1))
-        shared = ctx.enter_context(tc.tile_pool(name="shared", bufs=1))
         psum = ctx.enter_context(tc.psum_pool(name="psum", bufs=1))
 
         def load_list(name, src):
@@ -47,53 +46,52 @@ def tile_picked_dhlsendmxpagez_none_p_kernel(
             return tile
 
         x_scale_table = keep.tile([P, T], U8, name="x_scale_table", align_bytes=64)
-        w_scale_raw = keep.tile([P, 2 * H], U8, name="w_scale_raw", tag="w_scale_raw", align_bytes=64)
+        w_scale_raw = keep.tile([P, 2 * H], U8, name="w_scale_raw", align_bytes=64)
         nc.vector.memset(x_scale_table[:].bitcast(I32), 0)
-        nc.vector.memset(w_scale_raw[:].bitcast(I32), 0)
+        nc.gpsimd.memset(w_scale_raw[:].bitcast(I32), 0)
         zero = keep.tile([P, 1], F32, name="zero")
         nc.vector.memset(zero[:], 0.0)
 
-        x_table = keep.tile([P, T], U32, name="x_table", align_bytes=64)
+        w_raw = [keep.tile([P, H], U32, name=f"w_raw{w}", align_bytes=64) for w in range(2)]
+        nc.sync.dma_start(w_raw[0][:].bitcast(I32), words_of(w1_words))
         pick_lists = [load_list("offs_list", offs), load_list("hz_list", hz)]
-        nc.sync.dma_start(x_scale_table[0:P:STAGE_STEP, :].bitcast(I32), x_scales[0].bitcast(I32))
         for w, scales in enumerate((w1_scales, w2_scales)):
-            nc.sync.dma_start(w_scale_raw[0:P:STAGE_STEP, w * H : (w + 1) * H].bitcast(I32), scales[0].bitcast(I32))
-        send_list = load_list("n1_list", n1)
-        fetch_list = load_list("n3_list", n3)
+            nc.scalar.dma_start(w_scale_raw[0:P:STAGE_STEP, w * H : (w + 1) * H].bitcast(I32), scales[0].bitcast(I32))
+        for a in range(2):
+            nc.sync.dma_start(x_scale_table[a:P:GROUP, :].bitcast(I32), x_scales[0, a:16:2, :].bitcast(I32))
+        x_table = keep.tile([P, T], U32, name="x_table", align_bytes=64)
         nc.sync.dma_start(x_table[:].bitcast(I32), words_of(x_words))
-        page_list = load_list("n2_list", n2)
-        gain = keep.tile([P, PACK], F32, name="gain")
-        nc.gpsimd.dma_start(gain[:], gn.rearrange("(p t) o -> p (t o)", t=PACK))
-        w_raw = []
-        for w, words in enumerate((w1_words, w2_words)):
-            raw = keep.tile([P, H], U32, name=f"w_raw{w}", tag=f"w_raw{w}", align_bytes=64)
-            nc.sync.dma_start(raw[:].bitcast(I32), words_of(words))
-            w_raw.append(raw)
+        send_list = load_list("n1_list", n1)
+        nc.sync.dma_start(w_raw[1][:].bitcast(I32), words_of(w2_words))
 
-        first_page = keep.tile([P, U], F32, name="page0")
-        nc.scalar.activation(first_page[:], zero[:, 0:1].to_broadcast([P, U]), ACT.Copy)
+        pages = [keep.tile([P, U], F32, name=f"page{t}") for t in range(EARLY_PAGES)]
+        for page in pages:
+            nc.scalar.activation(page[:], zero[:, 0:1].to_broadcast([P, U]), ACT.Copy)
+        w3_scale = keep.tile([P, N], U8, name="w3_scale", align_bytes=64)
+        nc.vector.memset(w3_scale[:].bitcast(I32), 0)
         fetch_from = []
         for t in range(N // P):
             positive = keep.tile([P, FETCH_WINDOW], F32, name=f"positive{t}")
             nc.vector.memset(positive[:, S:], 0.0)
             fetch_from.append(positive)
 
+        w_scale = keep.tile([P, 2 * H], U8, name="w_scale", align_bytes=64)
+        for w in range(2):
+            nc.gpsimd.tensor_copy(
+                w_scale[:, w * H : (w + 1) * H].rearrange("p (t m) -> p t m", t=PACK),
+                w_scale_raw[:, w * H : (w + 1) * H].rearrange("p (m t) -> p t m", t=PACK),
+            )
+        for a in range(1, PACK):
+            nc.sync.dma_start(w_scale[a:P:QUAD, :].bitcast(I32), w_scale[STAGE_STEP * a : P : QUAD, :].bitcast(I32))
 
         picked_scale = keep.tile([P, 2 * S], U8, name="picked_scale", align_bytes=64)
         for w in range(2):
             nc.vector.tensor_copy(picked_scale[:, w * S : (w + 1) * S], x_scale_table[:].indirect(pick_lists[w][:]))
         x_scale = keep.tile([P, 2 * S], U8, name="x_scale", align_bytes=64)
         nc.vector.tensor_copy(x_scale[:].bitcast(I32), picked_scale[:].bitcast(I32))
-        for a in range(1, PACK):
-            nc.sync.dma_start(x_scale[a:P:QUAD, :].bitcast(I32), picked_scale[STAGE_STEP * a : P : QUAD, :].bitcast(I32))
+        for a in range(2):
+            nc.sync.dma_start(x_scale[2 + a : P : QUAD, :].bitcast(I32), picked_scale[GROUP + a : P : QUAD, :].bitcast(I32))
 
-        w_scale = keep.tile([P, 2 * H], U8, name="w_scale", align_bytes=64)
-        nc.vector.tensor_copy(
-            w_scale[:].rearrange("p (w t m) -> p w m t", w=2, t=PACK),
-            w_scale_raw[:].rearrange("p (w m t) -> p w m t", w=2, t=PACK),
-        )
-        for a in range(1, PACK):
-            nc.sync.dma_start(w_scale[a:P:QUAD, :].bitcast(I32), w_scale[STAGE_STEP * a : P : QUAD, :].bitcast(I32))
 
         picked = []
         for w in range(2):
@@ -102,47 +100,57 @@ def tile_picked_dhlsendmxpagez_none_p_kernel(
             picked.append(tile)
 
         w_codes = []
-        for w, (copy, word) in enumerate(((nc.scalar.copy, U32), (nc.vector.tensor_copy, I32))):
+        for w in range(2):
             dealt = keep.tile([P, H], U32, name=f"w_codes{w}", align_bytes=64)
-            copy(
-                dealt[:].bitcast(word).rearrange("p (t m) -> p m t", t=PACK),
-                w_raw[w][:].bitcast(word).rearrange("p (m t) -> p m t", t=PACK),
-            )
+            for tiles in (slice(0, 1), slice(1, PACK)) if w == 1 else (slice(0, PACK),):
+                nc.scalar.copy(
+                    dealt[:].rearrange("p (t m) -> p m t", t=PACK)[:, :, tiles],
+                    w_raw[w][:].rearrange("p (m t) -> p m t", t=PACK)[:, :, tiles],
+                )
             w_codes.append(dealt)
-        w3_codes = keep.tile([P, N], U32, name="w3_codes", tag="w_raw0", align_bytes=64)
+        gain = keep.tile([P, PACK], F32, name="gain")
+        nc.sync.dma_start(gain[:], gn.rearrange("(p t) o -> p (t o)", t=PACK))
         minus_gain = keep.tile([P, PACK], F32, name="minus_gain")
         nc.vector.tensor_scalar(minus_gain[:], gain[:], -1.0, None, ALU.mult)
-        w3_scale = keep.tile([P, N], U8, name="w3_scale", tag="w_scale_raw", align_bytes=64)
-        nc.vector.memset(w3_scale[:].bitcast(I32), 0)
         for a in range(PACK):
             nc.sync.dma_start(w3_scale[a:P:QUAD, :].bitcast(I32), w3_scales[0, a : 16 : PACK, :].bitcast(I32))
+        w3_codes = keep.tile([P, N], U32, name="w3_codes", align_bytes=64)
         nc.sync.dma_start(w3_codes[:].bitcast(I32), words_of(w3_words))
+        fetch_list = load_list("n3_list", n3)
+        page_list = load_list("n2_list", n2)
 
-        y_banks = [psum.tile([P, S], F32, name=f"y_bank{t}", tag=f"y_bank{t}") for t in range(PACK)]
+        y_parts = []
         for t in range(PACK):
-            for w in range(2):
-                nc.tensor.matmul_mx(
-                    out=y_banks[t][:],
-                    lhsT=w_codes[w][:, t * P : (t + 1) * P].bitcast(FP8X4),
-                    lhsT_scale=w_scale[:, w * H + t * P : w * H + (t + 1) * P],
-                    rhs=picked[w][:].bitcast(FP8X4),
-                    rhs_scale=x_scale[:, w * S : (w + 1) * S],
-                    start=(w == 0),
-                    stop=(w == 1),
-                )
+            parts = []
+            for cols in HALVES if t == 0 else WHOLE:
+                bank = psum.tile([P, cols.stop - cols.start], F32, name=f"y{t}_{cols.start}", tag=f"y{t}_{cols.start}")
+                for w in range(2):
+                    picked_cols = slice(w * S + cols.start, w * S + cols.stop)
+                    nc.tensor.matmul_mx(
+                        out=bank[:],
+                        lhsT=w_codes[w][:, t * P : (t + 1) * P].bitcast(FP8X4),
+                        lhsT_scale=w_scale[:, w * H + t * P : w * H + (t + 1) * P],
+                        rhs=picked[w][:, cols].bitcast(FP8X4),
+                        rhs_scale=x_scale[:, picked_cols],
+                        start=(w == 0),
+                        stop=(w == 1),
+                    )
+                parts.append((cols, bank))
+            y_parts.append(parts)
 
         z_words = keep.tile([P, S, PACK], BF16, name="z_words", align_bytes=64)
-        y_rows, y_gained, sent = [], [], []
+        y_gained, sent = [], []
         for t in range(PACK):
             y = keep.tile([P, S], F32, name=f"y{t}")
-            nc.vector.tensor_copy(y[:], y_banks[t][:])
+            for cols, bank in y_parts[t]:
+                nc.vector.tensor_copy(y[:, cols], bank[:])
             ds = keep.tile([P, SEND_WINDOW], F32, name=f"ds{t}")
             nc.scalar.activation(ds[:].indirect(send_list[:]), y[:], ACT.Copy)
-            y_rows.append(y)
             sent.append(ds)
         for t in range(PACK):
             gained = keep.tile([P, S], F32, name=f"gained{t}")
-            nc.vector.tensor_scalar(gained[:], y_banks[t][:], gain[:, t : t + 1], None, ALU.mult)
+            for cols, bank in y_parts[t]:
+                nc.vector.tensor_scalar(gained[:, cols], bank[:], gain[:, t : t + 1], None, ALU.mult)
             y_gained.append(gained)
         for t in range(PACK):
             for cols in HALVES if t == PACK - 1 else WHOLE:
@@ -150,8 +158,8 @@ def tile_picked_dhlsendmxpagez_none_p_kernel(
                     z_words[:, cols, t], sent[t][:, cols], minus_gain[:, t : t + 1], y_gained[t][:, cols], ALU.mult, ALU.add
                 )
 
-        z_codes = shared.tile([P, S], U32, name="z_codes", align_bytes=64, offset=PAGE_BYTES - Z_CODE_BYTES // 2)
-        z_scale = shared.tile([P, S], U8, name="z_scale", align_bytes=64, offset=2 * PAGE_BYTES)
+        z_codes = keep.tile([P, S], U32, name="z_codes", align_bytes=64)
+        z_scale = keep.tile([P, S], U8, name="z_scale", align_bytes=64)
         for cols in HALVES:
             nc.vector.quantize_mx(
                 out=z_codes[:, cols].bitcast(FP8X4),
@@ -163,7 +171,7 @@ def tile_picked_dhlsendmxpagez_none_p_kernel(
         for t in range(N // P):
             parts = []
             for cols in HALVES if t == 0 else WHOLE:
-                tag = "y_bank0" if cols.start else f"h_bank{t}"
+                tag = f"y0_{cols.start}" if t == 0 else f"h{t}"
                 bank = psum.tile([P, cols.stop - cols.start], F32, name=f"h{t}_{cols.start}", tag=tag)
                 nc.tensor.matmul_mx(
                     out=bank[:],
@@ -180,7 +188,7 @@ def tile_picked_dhlsendmxpagez_none_p_kernel(
         for t in range(N // P):
             for cols, bank in h_parts[t]:
                 nc.vector.tensor_scalar(fetch_from[t][:, cols], bank[:], 0.0, None, ALU.max)
-            got = keep.tile([P, S], F32, name=f"fetched{t}")
+            got = keep.tile([P, S], F32, name=f"fetched{t}", tag=f"fetched{t}")
             nc.scalar.activation(got[:], fetch_from[t][:].indirect(fetch_list[:]), ACT.Copy)
             fetched.append(got)
         results = []
@@ -189,9 +197,8 @@ def tile_picked_dhlsendmxpagez_none_p_kernel(
             for cols, bank in h_parts[t]:
                 nc.vector.tensor_tensor(nw[:, cols], bank[:], fetched[t][:, cols], ALU.subtract)
             results.append(nw)
-        pages = [first_page]
-        for t in range(1, N // P):
-            page = shared.tile([P, U], F32, name=f"page{t}", align_bytes=64, offset=(t - 1) * PAGE_BYTES)
+        for t in range(EARLY_PAGES, N // P):
+            page = keep.tile([P, U], F32, name=f"page{t}", tag=f"fetched{t - EARLY_PAGES}")
             nc.vector.memset(page[:], 0.0)
             pages.append(page)
         for t in range(N // P):

from contextlib import ExitStack

import concourse.mybir as mybir

K, T, S, N, H, U = 512, 2048, 256, 512, 512, 1024
FLOPS = 2 * (2 * K * H * S + H * N * S)

F32 = mybir.dt.float32
BF16 = mybir.dt.bfloat16
I32 = mybir.dt.int32
U32 = mybir.dt.uint32
U16 = mybir.dt.uint16
U8 = mybir.dt.uint8
FP8X4 = mybir.dt.float8_e4m3fn_x4
ALU = mybir.AluOpType
ACT = mybir.ActivationFunctionType

P = 128
PACK = 4
QUAD = 32
STAGE_STEP = 8
GROUP = 16
EARLY_PAGES = 2
SEND_WINDOW = 2 * S
FETCH_WINDOW = S + 16
WHOLE = (slice(0, S),)
HALVES = (slice(0, S // 2), slice(S // 2, S))


def words_of(packed):
    return packed[0].rearrange("p n t -> p (n t)").bitcast(I32)


def tile_picked_dhlsendmxpagez_none_p_kernel(
    tc, x_words, x_scales, w1_words, w1_scales, w2_words, w2_scales, gn, w3_words, w3_scales, offs, hz, n1, n2, n3, out
):
    nc = tc.nc
    with ExitStack() as ctx:
        lists = ctx.enter_context(tc.tile_pool(name="lists", bufs=1))
        keep = ctx.enter_context(tc.tile_pool(name="keep", bufs=1))
        psum = ctx.enter_context(tc.psum_pool(name="psum", bufs=1))

        def load_list(name, src):
            tile = lists.tile([P, S // 16], U16, name=name)
            nc.sync.dma_start(tile[:], src)
            return tile

        x_scale_table = keep.tile([P, T], U8, name="x_scale_table", align_bytes=64)
        w_scale_raw = keep.tile([P, 2 * H], U8, name="w_scale_raw", align_bytes=64)
        nc.vector.memset(x_scale_table[:].bitcast(I32), 0)
        nc.gpsimd.memset(w_scale_raw[:].bitcast(I32), 0)
        zero = keep.tile([P, 1], F32, name="zero")
        nc.vector.memset(zero[:], 0.0)

        w_raw = [keep.tile([P, H], U32, name=f"w_raw{w}", align_bytes=64) for w in range(2)]
        nc.sync.dma_start(w_raw[0][:].bitcast(I32), words_of(w1_words))
        pick_lists = [load_list("offs_list", offs), load_list("hz_list", hz)]
        for w, scales in enumerate((w1_scales, w2_scales)):
            nc.scalar.dma_start(w_scale_raw[0:P:STAGE_STEP, w * H : (w + 1) * H].bitcast(I32), scales[0].bitcast(I32))
        for a in range(2):
            nc.sync.dma_start(x_scale_table[a:P:GROUP, :].bitcast(I32), x_scales[0, a:16:2, :].bitcast(I32))
        x_table = keep.tile([P, T], U32, name="x_table", align_bytes=64)
        nc.sync.dma_start(x_table[:].bitcast(I32), words_of(x_words))
        send_list = load_list("n1_list", n1)
        nc.sync.dma_start(w_raw[1][:].bitcast(I32), words_of(w2_words))

        pages = [keep.tile([P, U], F32, name=f"page{t}") for t in range(EARLY_PAGES)]
        for page in pages:
            nc.scalar.activation(page[:], zero[:, 0:1].to_broadcast([P, U]), ACT.Copy)
        w3_scale = keep.tile([P, N], U8, name="w3_scale", align_bytes=64)
        nc.vector.memset(w3_scale[:].bitcast(I32), 0)
        fetch_from = []
        for t in range(N // P):
            positive = keep.tile([P, FETCH_WINDOW], F32, name=f"positive{t}")
            nc.vector.memset(positive[:, S:], 0.0)
            fetch_from.append(positive)

        w_scale = keep.tile([P, 2 * H], U8, name="w_scale", align_bytes=64)
        for w in range(2):
            nc.gpsimd.tensor_copy(
                w_scale[:, w * H : (w + 1) * H].rearrange("p (t m) -> p t m", t=PACK),
                w_scale_raw[:, w * H : (w + 1) * H].rearrange("p (m t) -> p t m", t=PACK),
            )
        for a in range(1, PACK):
            nc.sync.dma_start(w_scale[a:P:QUAD, :].bitcast(I32), w_scale[STAGE_STEP * a : P : QUAD, :].bitcast(I32))

        picked_scale = keep.tile([P, 2 * S], U8, name="picked_scale", align_bytes=64)
        for w in range(2):
            nc.vector.tensor_copy(picked_scale[:, w * S : (w + 1) * S], x_scale_table[:].indirect(pick_lists[w][:]))
        x_scale = keep.tile([P, 2 * S], U8, name="x_scale", align_bytes=64)
        nc.vector.tensor_copy(x_scale[:].bitcast(I32), picked_scale[:].bitcast(I32))
        for a in range(2):
            nc.sync.dma_start(x_scale[2 + a : P : QUAD, :].bitcast(I32), picked_scale[GROUP + a : P : QUAD, :].bitcast(I32))


        picked = []
        for w in range(2):
            tile = keep.tile([P, S], U32, name=f"picked{w}", align_bytes=64)
            nc.vector.tensor_copy(tile[:], x_table[:].indirect(pick_lists[w][:]))
            picked.append(tile)

        w_codes = []
        for w in range(2):
            dealt = keep.tile([P, H], U32, name=f"w_codes{w}", align_bytes=64)
            for tiles in (slice(0, 1), slice(1, PACK)) if w == 1 else (slice(0, PACK),):
                nc.scalar.copy(
                    dealt[:].rearrange("p (t m) -> p m t", t=PACK)[:, :, tiles],
                    w_raw[w][:].rearrange("p (m t) -> p m t", t=PACK)[:, :, tiles],
                )
            w_codes.append(dealt)
        gain = keep.tile([P, PACK], F32, name="gain")
        nc.sync.dma_start(gain[:], gn.rearrange("(p t) o -> p (t o)", t=PACK))
        minus_gain = keep.tile([P, PACK], F32, name="minus_gain")
        nc.vector.tensor_scalar(minus_gain[:], gain[:], -1.0, None, ALU.mult)
        for a in range(PACK):
            nc.sync.dma_start(w3_scale[a:P:QUAD, :].bitcast(I32), w3_scales[0, a : 16 : PACK, :].bitcast(I32))
        w3_codes = keep.tile([P, N], U32, name="w3_codes", align_bytes=64)
        nc.sync.dma_start(w3_codes[:].bitcast(I32), words_of(w3_words))
        fetch_list = load_list("n3_list", n3)
        page_list = load_list("n2_list", n2)

        y_parts = []
        for t in range(PACK):
            parts = []
            for cols in HALVES if t == 0 else WHOLE:
                bank = psum.tile([P, cols.stop - cols.start], F32, name=f"y{t}_{cols.start}", tag=f"y{t}_{cols.start}")
                for w in range(2):
                    picked_cols = slice(w * S + cols.start, w * S + cols.stop)
                    nc.tensor.matmul_mx(
                        out=bank[:],
                        lhsT=w_codes[w][:, t * P : (t + 1) * P].bitcast(FP8X4),
                        lhsT_scale=w_scale[:, w * H + t * P : w * H + (t + 1) * P],
                        rhs=picked[w][:, cols].bitcast(FP8X4),
                        rhs_scale=x_scale[:, picked_cols],
                        start=(w == 0),
                        stop=(w == 1),
                    )
                parts.append((cols, bank))
            y_parts.append(parts)

        z_words = keep.tile([P, S, PACK], BF16, name="z_words", align_bytes=64)
        y_gained, sent = [], []
        for t in range(PACK):
            y = keep.tile([P, S], F32, name=f"y{t}")
            for cols, bank in y_parts[t]:
                nc.vector.tensor_copy(y[:, cols], bank[:])
            ds = keep.tile([P, SEND_WINDOW], F32, name=f"ds{t}")
            nc.scalar.activation(ds[:].indirect(send_list[:]), y[:], ACT.Copy)
            sent.append(ds)
        for t in range(PACK):
            gained = keep.tile([P, S], F32, name=f"gained{t}")
            for cols, bank in y_parts[t]:
                nc.vector.tensor_scalar(gained[:, cols], bank[:], gain[:, t : t + 1], None, ALU.mult)
            y_gained.append(gained)
        for t in range(PACK):
            for cols in HALVES if t == PACK - 1 else WHOLE:
                nc.vector.scalar_tensor_tensor(
                    z_words[:, cols, t], sent[t][:, cols], minus_gain[:, t : t + 1], y_gained[t][:, cols], ALU.mult, ALU.add
                )

        z_codes = keep.tile([P, S], U32, name="z_codes", align_bytes=64)
        z_scale = keep.tile([P, S], U8, name="z_scale", align_bytes=64)
        for cols in HALVES:
            nc.vector.quantize_mx(
                out=z_codes[:, cols].bitcast(FP8X4),
                scales=z_scale[:, cols],
                in_=z_words[:, cols, :].rearrange("p j t -> p (j t)"),
            )

        h_parts = []
        for t in range(N // P):
            parts = []
            for cols in HALVES if t == 0 else WHOLE:
                tag = f"y0_{cols.start}" if t == 0 else f"h{t}"
                bank = psum.tile([P, cols.stop - cols.start], F32, name=f"h{t}_{cols.start}", tag=tag)
                nc.tensor.matmul_mx(
                    out=bank[:],
                    lhsT=w3_codes[:, t * P : (t + 1) * P].bitcast(FP8X4),
                    lhsT_scale=w3_scale[:, t * P : (t + 1) * P],
                    rhs=z_codes[:, cols].bitcast(FP8X4),
                    rhs_scale=z_scale[:, cols],
                    start=True,
                    stop=True,
                )
                parts.append((cols, bank))
            h_parts.append(parts)
        fetched = []
        for t in range(N // P):
            for cols, bank in h_parts[t]:
                nc.vector.tensor_scalar(fetch_from[t][:, cols], bank[:], 0.0, None, ALU.max)
            got = keep.tile([P, S], F32, name=f"fetched{t}", tag=f"fetched{t}")
            nc.scalar.activation(got[:], fetch_from[t][:].indirect(fetch_list[:]), ACT.Copy)
            fetched.append(got)
        results = []
        for t in range(N // P):
            nw = keep.tile([P, S], F32, name=f"nw{t}")
            for cols, bank in h_parts[t]:
                nc.vector.tensor_tensor(nw[:, cols], bank[:], fetched[t][:, cols], ALU.subtract)
            results.append(nw)
        for t in range(EARLY_PAGES, N // P):
            page = keep.tile([P, U], F32, name=f"page{t}", tag=f"fetched{t - EARLY_PAGES}")
            nc.vector.memset(page[:], 0.0)
            pages.append(page)
        for t in range(N // P):
            nw = results[t]
            nc.scalar.activation(pages[t][:].indirect(page_list[:]), nw[:], ACT.Copy)
            nc.sync.dma_start(out[t * P : (t + 1) * P, :], pages[t][:])
